import numpy as np
import ml_dtypes


def mxq(x, axis, fmt="e4m3"):
    dtype, down = {"e4m3": (ml_dtypes.float8_e4m3fn, 7), "e5m2": (ml_dtypes.float8_e5m2, 14)}[fmt]
    v = np.moveaxis(np.asarray(x, np.float32).astype(ml_dtypes.bfloat16).astype(np.float64), axis, -1)
    blocks = v.reshape(v.shape[:-1] + (-1, 32))
    amax = np.abs(blocks).max(-1, keepdims=True)
    byte = np.maximum(np.where(amax > 0, np.frexp(amax)[1] - 1 + 127, 0) - down, 1)
    scale = np.exp2(byte - 127.0)
    codes = (blocks / scale).astype(np.float32).astype(dtype).astype(np.float64)
    return np.moveaxis((codes * scale).reshape(v.shape), -1, axis)


WIDE = False


def mx_kscale(k):
    if not WIDE:
        return np.ones(k)
    levels = np.array([10, -10, 5, -5, 0])
    if k % 512:
        return np.exp2(np.random.permutation(np.resize(levels, k // 32))).repeat(32)
    a = np.empty((k // 512, 16))
    for p in range(k // 512):
        a[p, :8] = np.random.permutation(np.resize(levels, 8))
        for g in range(8):
            far = levels[np.abs(levels - a[p, g]) >= 10]
            a[p, g + 8] = far[np.random.randint(len(far))]
    return np.exp2(a.ravel()).repeat(32)


def f64(x):
    return np.asarray(x).astype(np.float64)


def striped(idx):
    return np.tile(np.asarray(idx).reshape(-1, 16).T, (8, 1)).astype(np.uint16)


def unstriped(offs):
    return offs[:16].T.reshape(-1).astype(np.int64)


def striped8(idx):
    return np.asarray(idx).reshape(8, -1, 16).transpose(0, 2, 1).reshape(128, -1).astype(np.uint16)


def unstriped8(offs):
    return offs.reshape(8, 16, -1).transpose(0, 2, 1).reshape(8, -1).astype(np.int64)


def pick8(x, idx, run):
    r = np.arange(len(x))
    return x[r[:, None], idx[r % (8 * run) // run]]


E2M1 = np.array([0.0, 0.5, 1.0, 1.5, 2.0, 3.0, 4.0, 6.0, -0.0, -0.5, -1.0, -1.5, -2.0, -3.0, -4.0, -6.0])


def pack_weight(w, fmt):
    k, n = w.shape
    w = f64(np.asarray(w, np.float32).astype(ml_dtypes.bfloat16)).reshape(k // 32, 32, n)
    amax = np.abs(w).max(1)
    if fmt == "e4m3":
        byte = np.frexp(amax)[1] - 1 + 127 - 7
    else:
        mant, ex = np.frexp(amax / 6.0)
        byte = np.where(mant > 0.5, ex, ex - 1) + 127
    byte = np.clip(np.where(amax > 0, byte, 1), 1, 254)
    scaled = (w * np.exp2(127.0 - byte)[:, None, :]).reshape(k, n).astype(np.float32)
    by_word = np.ascontiguousarray(scaled.reshape(k // 512, 128, 4, n).transpose(0, 1, 3, 2))
    if fmt == "e4m3":
        words = by_word.astype(ml_dtypes.float8_e4m3fn).view(np.uint8)
    else:
        c = by_word.astype(ml_dtypes.float4_e2m1fn).view(np.uint8) & 0xF
        words = (c[..., 0::2] | (c[..., 1::2] << 4)).reshape(k // 512, 128, 2 * n)
    return np.ascontiguousarray(words), np.ascontiguousarray(byte.astype(np.uint8).reshape(k // 512, 16, n))


def unpack_weight(words, scales, fmt):
    g, _, n = scales.shape
    words = np.ascontiguousarray(words).reshape(g, 128, n, -1)
    if fmt == "e4m3":
        vals = words.view(ml_dtypes.float8_e4m3fn).astype(np.float64)
    else:
        nib = np.empty((g, 128, n, 4), np.uint8)
        nib[..., 0::2] = words & 0xF
        nib[..., 1::2] = words >> 4
        vals = E2M1[nib]
    vals = vals * np.repeat(np.exp2(scales.astype(np.float64) - 127.0), 8, axis=1)[..., None]
    return vals.transpose(0, 1, 3, 2).reshape(g * 512, n)


def sigmoid(v):
    return 1.0 / (1.0 + np.exp(-v))


K, R, F, T, J, U, M = 512, 128, 512, 2048, 512, 1024, 256


def setup_inputs():
    n = np.random.standard_normal
    idx = np.random.permutation(T)[:J]
    idx2 = np.stack([np.random.permutation(U)[:J] for _ in range(8)])
    idx3 = np.stack([np.random.permutation(U)[:M] for _ in range(8)])
    fk = mx_kscale(K)
    ff = mx_kscale(F)
    tabp = pack_weight(n((K, T)) / fk[:, None], "e2m1")
    dtabp = pack_weight(n((K, T)) / fk[:, None], "e2m1")
    return {
        "tab_words": tabp[0],
        "tab_scales": tabp[1],
        "w1": (n((K, R)) * 1 / np.sqrt(K) * fk[:, None]).astype(np.float32),
        "gain": (np.random.uniform(0.5, 1.5, (R, 1))).astype(np.float32),
        "pb": (np.random.uniform(0.3, 1.0, (1, M))).astype(np.float32),
        "wo": (n((F, R)) * 1 / np.sqrt(F) * ff[:, None]).astype(np.float32),
        "dy": (n((F, M)) / ff[:, None]).astype(np.float32),
        "dtab_words": dtabp[0],
        "dtab_scales": dtabp[1],
        "og": (np.random.uniform(0.7, 2.0, (R, 1))).astype(np.float32),
        "base": (0.3 * n((R, J))).astype(np.float32),
        "offs": striped(idx),
        "offs2": striped8(idx2),
        "offs3": striped8(idx3),
    }


def reference(tab_words, tab_scales, w1, gain, pb, wo, dy, dtab_words, dtab_scales, og, base, offs, offs2, offs3):
    idx = unstriped(offs)
    idx2 = unstriped8(offs2)
    idx3 = unstriped8(offs3)
    tabu = unpack_weight(tab_words, tab_scales, "e2m1")
    dtabu = unpack_weight(dtab_words, dtab_scales, "e2m1")
    w1q = mxq(f64(w1), 0, "e4m3")
    tabidxg = tabu[:, idx]
    a = w1q.T @ tabidxg
    dtabidxg = dtabu[:, idx]
    ta = w1q.T @ dtabidxg
    h1 = np.tanh(a)
    h2 = h1 * f64(gain)
    pg = np.zeros((R, U))
    pg[np.arange(R)[:, None], idx2[np.arange(R) % 128 // 16]] = h2
    s = pick8(pg, idx3, 16) + f64(pb)
    woq = mxq(f64(wo), 0, "e4m3")
    dyq = mxq(f64(dy), 0, "e4m3")
    c0 = woq.T @ dyq
    ds = c0 * sigmoid(s) + c0 * s * sigmoid(s) * (1.0 - sigmoid(s))
    s1 = np.zeros((R, U))
    s1[np.arange(R)[:, None], idx3[np.arange(R) % 128 // 16]] = ds
    dh2 = pick8(s1, idx2, 16)
    dh1 = dh2 * f64(gain)
    xh1 = ta * (1.0 - np.square(h1))
    xh2 = xh1 * f64(gain)
    xpg = np.zeros((R, U))
    xpg[np.arange(R)[:, None], idx2[np.arange(R) % 128 // 16]] = xh2
    xs = pick8(xpg, idx3, 16)
    xds = xs * sigmoid(s) * (1.0 - sigmoid(s)) * c0 + (xs * c0 * sigmoid(s) + xs * sigmoid(s) * (1.0 - sigmoid(s)) * c0 * s) * (1.0 - sigmoid(s)) + xs * sigmoid(s) * (1.0 - sigmoid(s)) * (-1.0) * c0 * s * sigmoid(s)
    xs1 = np.zeros((R, U))
    xs1[np.arange(R)[:, None], idx3[np.arange(R) % 128 // 16]] = xds
    xdh2 = pick8(xs1, idx2, 16)
    xdh1 = xdh2 * f64(gain)
    xda = xdh1 * (1.0 - np.square(h1)) + xh1 * h1 * 2.0 * (-1.0) * dh1
    y = xda * f64(og) + f64(base)
    return y

@@ -1,0 +1,178 @@
+from contextlib import ExitStack
+
+import concourse.mybir as mybir
+
+K, R, F, T, J, U, M = 512, 128, 512, 2048, 512, 1024, 256
+P = 128
+PACK = 4
+HALF = J // 2
+
+FLOPS = 2 * K * R * J * 2 + 2 * F * R * M
+
+F32 = mybir.dt.float32
+BF16 = mybir.dt.bfloat16
+I32 = mybir.dt.int32
+U32 = mybir.dt.uint32
+U16 = mybir.dt.uint16
+U8 = mybir.dt.uint8
+FP8X4 = mybir.dt.float8_e4m3fn_x4
+FP4X4 = mybir.dt.float4_e2m1fn_x4
+ALU = mybir.AluOpType
+ACT = mybir.ActivationFunctionType
+
+
+def tile_attend_hvwriteread_kernel(tc, tab_words, tab_scales, w1, gain, pb, wo, dy, dtab_words, dtab_scales,
+                                    og, base, offs, offs2, offs3, out):
+    nc = tc.nc
+    with ExitStack() as ctx:
+        pool = ctx.enter_context(tc.tile_pool(name="sbuf", bufs=1))
+        psum = ctx.enter_context(tc.psum_pool(name="psum", bufs=1))
+
+        def sb(name, shape, dtype):
+            return pool.tile(shape, dtype, name=name, align_bytes=64)
+
+        def load_words(name, words):
+            window = sb(name, [P, T], U16)
+            nc.sync.dma_start(out=window[:].bitcast(I32), in_=words[0].bitcast(I32))
+            return window
+
+        def load_scales(queue, window, scales):
+            for row in range(4):
+                queue.dma_start(out=window[row:P:32, :].bitcast(I32), in_=scales[0, row:16:4, :].bitcast(I32))
+
+        def load_rows(name, rows):
+            raw = sb(name, [P, PACK, rows.shape[1]], F32)
+            nc.sync.dma_start(out=raw[:], in_=rows.rearrange("(p t) c -> p t c", t=PACK))
+            return raw
+
+        def load_plain(name, src, dtype, queue=nc.sync):
+            tile = sb(name, list(src.shape), dtype)
+            queue.dma_start(out=tile[:], in_=src)
+            return tile
+
+        def interleave(name, raw):
+            grouped = sb(name, [P, raw.shape[2], PACK], BF16)
+            nc.scalar.copy(out=grouped[:], in_=raw[:].rearrange("p t c -> p c t"))
+            return grouped
+
+        def quantise(name, grouped):
+            width = grouped.shape[1]
+            codes = sb(name + "_codes", [P, width], U32)
+            scales = sb(name + "_scales", [P, width], U8)
+            nc.vector.quantize_mx(out=codes[:].bitcast(FP8X4), scales=scales[:],
+                                  in_=grouped[:].rearrange("p c t -> p (c t)"))
+            return codes, scales
+
+        def gather_packed(name, window, dtype):
+            picked = sb(name, [P, J], dtype)
+            nc.vector.tensor_copy(out=picked[:], in_=window[:].indirect(list1[:]))
+            return picked
+
+        def affine(name, src, scale, bias=0.0):
+            dst = sb(name, list(src.shape), F32)
+            nc.scalar.activation(out=dst[:], in_=src, func=ACT.Copy, scale=scale, bias=bias)
+            return dst
+
+        tab_scale_win = sb("tab_scale_win", [P, T], U8)
+        dtab_scale_win = sb("dtab_scale_win", [P, T], U8)
+        nc.vector.memset(tab_scale_win[:].bitcast(I32), 0)
+        nc.vector.memset(dtab_scale_win[:].bitcast(I32), 0)
+        pages = {}
+        for name in ("pg", "xpg", "s1", "xs1"):
+            pages[name] = sb(name, [P, U], F32)
+            nc.vector.memset(pages[name][:], 0.0)
+
+        list1 = load_plain("list1", offs, U16)
+        tab_word_win = load_words("tab_word_win", tab_words)
+        w1_raw = load_rows("w1_raw", w1)
+        load_scales(nc.sync, tab_scale_win, tab_scales)
+        dtab_word_win = load_words("dtab_word_win", dtab_words)
+        load_scales(nc.sync, dtab_scale_win, dtab_scales)
+        list2 = load_plain("list2", offs2, U16)
+        gain_col = load_plain("gain_col", gain, F32, nc.gpsimd)
+        wo_raw = load_rows("wo_raw", wo)
+        dy_raw = load_rows("dy_raw", dy)
+        list3 = load_plain("list3", offs3, U16)
+        og_col = load_plain("og_col", og, F32, nc.gpsimd)
+        pb_rows = sb("pb_rows", [P, M], F32)
+        nc.sync.dma_start(out=pb_rows[:], in_=pb[0].partition_broadcast(P))
+        base_sb = load_plain("base_sb", base, F32)
+
+        w1_grouped = interleave("w1_grouped", w1_raw)
+        tab_picked_words = gather_packed("tab_picked_words", tab_word_win, U16)
+        tab_picked_scales = gather_packed("tab_picked_scales", tab_scale_win, U8)
+        w1_codes, w1_scales = quantise("w1", w1_grouped)
+
+        def first_layer(name, words, scales):
+            acc = psum.tile([P, J], F32, name=name)
+            nc.tensor.matmul_mx(out=acc[:], lhsT=w1_codes[:].bitcast(FP8X4), lhsT_scale=w1_scales[:],
+                                rhs=words[:].bitcast(FP4X4), rhs_scale=scales[:], start=True, stop=True)
+            return acc
+
+        a = first_layer("a", tab_picked_words, tab_picked_scales)
+        dtab_picked_words = gather_packed("dtab_picked_words", dtab_word_win, U16)
+        dtab_picked_scales = gather_packed("dtab_picked_scales", dtab_scale_win, U8)
+        ta = first_layer("ta", dtab_picked_words, dtab_picked_scales)
+
+        gain_rows = affine("gain_rows", gain_col[:].to_broadcast([P, J]), 1.0)
+        h1 = sb("h1", [P, J], F32)
+        nc.scalar.activation(out=h1[:], in_=a[:], func=ACT.Tanh)
+        nc.vector.tensor_tensor(out=pages["pg"][:].indirect(list2[:]), in0=h1[:], in1=gain_rows[:], op=ALU.mult)
+
+        h1_sq = sb("h1_sq", [P, J], F32)
+        nc.scalar.activation(out=h1_sq[:], in_=h1[:], func=ACT.Square)
+        slope = affine("slope", h1_sq[:], -1.0, 1.0)
+        ta_gain = affine("ta_gain", ta[:], gain_col[:])
+        wo_grouped = interleave("wo_grouped", wo_raw)
+        dy_grouped = interleave("dy_grouped", dy_raw)
+
+        curv = sb("gain_rows", [P, J], F32)
+        nc.vector.scalar_tensor_tensor(out=curv[:], in0=ta[:], scalar=-2.0, in1=h1[:], op0=ALU.mult, op1=ALU.mult)
+        s = sb("s", [P, M], F32)
+        nc.vector.tensor_tensor(out=s[:], in0=pages["pg"][:].indirect(list3[:]), in1=pb_rows[:], op=ALU.add)
+        wo_codes, wo_scales = quantise("wo", wo_grouped)
+        dy_codes, dy_scales = quantise("dy", dy_grouped)
+        c0 = psum.tile([P, M], F32, name="c0")
+        nc.tensor.matmul_mx(out=c0[:], lhsT=wo_codes[:].bitcast(FP8X4), lhsT_scale=wo_scales[:],
+                            rhs=dy_codes[:].bitcast(FP8X4), rhs_scale=dy_scales[:], start=True, stop=True)
+        nc.vector.tensor_tensor(out=pages["xpg"][:].indirect(list2[:]), in0=ta_gain[:], in1=slope[:], op=ALU.mult)
+
+        neg_silu = sb("neg_silu", [P, M], F32)
+        nc.scalar.activation(out=neg_silu[:], in_=s[:], func=ACT.Silu, scale=-1.0)
+        th = sb("th", [P, M], F32)
+        nc.scalar.activation(out=th[:], in_=s[:], func=ACT.Tanh, scale=0.5)
+        half_q = affine("half_q", neg_silu[:], -0.5, 0.5)
+        out_gain = affine("out_gain", gain_col[:], og_col[:])
+        out_slope = affine("out_slope", slope[:], out_gain[:])
+
+        c_sig2 = sb("c_sig2", [P, M], F32)
+        nc.vector.scalar_tensor_tensor(out=c_sig2[:], in0=th[:], scalar=1.0, in1=c0[:], op0=ALU.add, op1=ALU.mult)
+        e_less1 = sb("e_less1", [P, M], F32)
+        nc.vector.scalar_tensor_tensor(out=e_less1[:], in0=neg_silu[:], scalar=-1.0, in1=th[:], op0=ALU.add, op1=ALU.mult)
+        half_e = affine("half_e", e_less1[:], 0.5, 0.5)
+        nc.vector.tensor_tensor(out=pages["s1"][:].indirect(list3[:]), in0=c_sig2[:], in1=half_q[:], op=ALU.mult)
+        xs_c = sb("xs_c", [P, M], F32)
+        nc.vector.tensor_tensor(out=xs_c[:], in0=pages["xpg"][:].indirect(list3[:]), in1=c_sig2[:], op=ALU.mult)
+
+        halves = [slice(h * HALF, (h + 1) * HALF) for h in range(2)]
+        half_lists = [list2[:, h * HALF // 16:(h + 1) * HALF // 16] for h in range(2)]
+        second = [sb("second%d" % h, [P, HALF], F32) for h in range(2)]
+        both = [sb("both%d" % h, [P, HALF], F32) for h in range(2)]
+        scaled = [sb("scaled%d" % h, [P, HALF], F32) for h in range(2)]
+        result = [sb("result%d" % h, [P, HALF], F32) for h in range(2)]
+
+        def second_term(h):
+            nc.vector.tensor_tensor(out=second[h][:], in0=pages["s1"][:].indirect(half_lists[h]),
+                                    in1=curv[:, halves[h]], op=ALU.mult)
+
+        second_term(0)
+        nc.vector.tensor_tensor(out=pages["xs1"][:].indirect(list3[:]), in0=xs_c[:], in1=half_e[:], op=ALU.mult)
+        second_term(1)
+        for h in range(2):
+            nc.vector.tensor_tensor(out=both[h][:], in0=pages["xs1"][:].indirect(half_lists[h]),
+                                    in1=second[h][:], op=ALU.add)
+        for h in range(2):
+            nc.vector.tensor_tensor(out=scaled[h][:], in0=both[h][:], in1=out_slope[:, halves[h]], op=ALU.mult)
+        for h in range(2):
+            nc.vector.tensor_tensor(out=result[h][:], in0=scaled[h][:], in1=base_sb[:, halves[h]], op=ALU.add)
+            nc.sync.dma_start(out=out[:, halves[h]], in_=result[h][:])

@@ -1,6 +1,7 @@
 from contextlib import ExitStack
 
 import concourse.mybir as mybir
+from concourse.masks import make_identity
 
 K, R, F, T, J, U, M = 512, 128, 512, 2048, 512, 1024, 256
 P = 128
@@ -78,7 +79,7 @@ def tile_attend_hvwriteread_kernel(tc, tab_words, tab_scales, w1, gain, pb, wo, 
         nc.vector.memset(tab_scale_win[:].bitcast(I32), 0)
         nc.vector.memset(dtab_scale_win[:].bitcast(I32), 0)
         pages = {}
-        for name in ("pg", "xpg", "s1", "xs1"):
+        for name in ("pg", "s1", "xs1"):
             pages[name] = sb(name, [P, U], F32)
             nc.vector.memset(pages[name][:], 0.0)
 
@@ -86,16 +87,15 @@ def tile_attend_hvwriteread_kernel(tc, tab_words, tab_scales, w1, gain, pb, wo, 
         tab_word_win = load_words("tab_word_win", tab_words)
         w1_raw = load_rows("w1_raw", w1)
         load_scales(nc.sync, tab_scale_win, tab_scales)
+        gain_col = load_plain("gain_col", gain, F32)
         dtab_word_win = load_words("dtab_word_win", dtab_words)
         load_scales(nc.sync, dtab_scale_win, dtab_scales)
         list2 = load_plain("list2", offs2, U16)
-        gain_col = load_plain("gain_col", gain, F32, nc.gpsimd)
-        wo_raw = load_rows("wo_raw", wo)
         dy_raw = load_rows("dy_raw", dy)
+        wo_raw = load_rows("wo_raw", wo)
         list3 = load_plain("list3", offs3, U16)
-        og_col = load_plain("og_col", og, F32, nc.gpsimd)
-        pb_rows = sb("pb_rows", [P, M], F32)
-        nc.sync.dma_start(out=pb_rows[:], in_=pb[0].partition_broadcast(P))
+        pb_cols = load_plain("pb_cols", pb[0].rearrange("(p c) -> p c", p=P), F32)
+        og_col = load_plain("og_col", og, F32)
         base_sb = load_plain("base_sb", base, F32)
 
         w1_grouped = interleave("w1_grouped", w1_raw)
@@ -123,19 +123,27 @@ def tile_attend_hvwriteread_kernel(tc, tab_words, tab_scales, w1, gain, pb, wo, 
         nc.scalar.activation(out=h1_sq[:], in_=h1[:], func=ACT.Square)
         slope = affine("slope", h1_sq[:], -1.0, 1.0)
         ta_gain = affine("ta_gain", ta[:], gain_col[:])
-        wo_grouped = interleave("wo_grouped", wo_raw)
         dy_grouped = interleave("dy_grouped", dy_raw)
+        wo_grouped = interleave("wo_grouped", wo_raw)
 
-        curv = sb("gain_rows", [P, J], F32)
-        nc.vector.scalar_tensor_tensor(out=curv[:], in0=ta[:], scalar=-2.0, in1=h1[:], op0=ALU.mult, op1=ALU.mult)
-        s = sb("s", [P, M], F32)
-        nc.vector.tensor_tensor(out=s[:], in0=pages["pg"][:].indirect(list3[:]), in1=pb_rows[:], op=ALU.add)
-        wo_codes, wo_scales = quantise("wo", wo_grouped)
+        identity = sb("identity", [P, P], F32)
+        make_identity(nc, identity[:])
+        pb_turned = psum.tile([P, M // P, P], F32, name="pb_turned")
+        for c in range(M // P):
+            nc.tensor.transpose(pb_turned[:, c, :], pb_cols[:, c:c + 1].to_broadcast([P, P]), identity[:])
+        pb_rows = sb("pb_rows", [P, M], F32)
+        nc.scalar.copy(out=pb_rows[:].rearrange("p (n c) -> p n c", c=M // P), in_=pb_turned[:].rearrange("p c n -> p n c"))
+
         dy_codes, dy_scales = quantise("dy", dy_grouped)
+        wo_codes, wo_scales = quantise("wo", wo_grouped)
+        s = sb("dy_grouped", [P, M], F32)
+        nc.vector.tensor_tensor(out=s[:], in0=pages["pg"][:].indirect(list3[:]), in1=pb_rows[:], op=ALU.add)
+        curv = sb("wo_grouped", [P, J], F32)
+        nc.vector.scalar_tensor_tensor(out=curv[:], in0=ta[:], scalar=-2.0, in1=h1[:], op0=ALU.mult, op1=ALU.mult)
         c0 = psum.tile([P, M], F32, name="c0")
         nc.tensor.matmul_mx(out=c0[:], lhsT=wo_codes[:].bitcast(FP8X4), lhsT_scale=wo_scales[:],
                             rhs=dy_codes[:].bitcast(FP8X4), rhs_scale=dy_scales[:], start=True, stop=True)
-        nc.vector.tensor_tensor(out=pages["xpg"][:].indirect(list2[:]), in0=ta_gain[:], in1=slope[:], op=ALU.mult)
+        nc.vector.tensor_tensor(out=pages["pg"][:].indirect(list2[:]), in0=ta_gain[:], in1=slope[:], op=ALU.mult)
 
         neg_silu = sb("neg_silu", [P, M], F32)
         nc.scalar.activation(out=neg_silu[:], in_=s[:], func=ACT.Silu, scale=-1.0)
@@ -152,25 +160,19 @@ def tile_attend_hvwriteread_kernel(tc, tab_words, tab_scales, w1, gain, pb, wo, 
         half_e = affine("half_e", e_less1[:], 0.5, 0.5)
         nc.vector.tensor_tensor(out=pages["s1"][:].indirect(list3[:]), in0=c_sig2[:], in1=half_q[:], op=ALU.mult)
         xs_c = sb("xs_c", [P, M], F32)
-        nc.vector.tensor_tensor(out=xs_c[:], in0=pages["xpg"][:].indirect(list3[:]), in1=c_sig2[:], op=ALU.mult)
+        nc.vector.tensor_tensor(out=xs_c[:], in0=pages["pg"][:].indirect(list3[:]), in1=c_sig2[:], op=ALU.mult)
 
         halves = [slice(h * HALF, (h + 1) * HALF) for h in range(2)]
         half_lists = [list2[:, h * HALF // 16:(h + 1) * HALF // 16] for h in range(2)]
-        second = [sb("second%d" % h, [P, HALF], F32) for h in range(2)]
         both = [sb("both%d" % h, [P, HALF], F32) for h in range(2)]
         scaled = [sb("scaled%d" % h, [P, HALF], F32) for h in range(2)]
         result = [sb("result%d" % h, [P, HALF], F32) for h in range(2)]
-
-        def second_term(h):
-            nc.vector.tensor_tensor(out=second[h][:], in0=pages["s1"][:].indirect(half_lists[h]),
-                                    in1=curv[:, halves[h]], op=ALU.mult)
-
-        second_term(0)
+        second = sb("second", [P, J], F32)
+        nc.vector.tensor_tensor(out=second[:], in0=pages["s1"][:].indirect(list2[:]), in1=curv[:], op=ALU.mult)
         nc.vector.tensor_tensor(out=pages["xs1"][:].indirect(list3[:]), in0=xs_c[:], in1=half_e[:], op=ALU.mult)
-        second_term(1)
         for h in range(2):
             nc.vector.tensor_tensor(out=both[h][:], in0=pages["xs1"][:].indirect(half_lists[h]),
-                                    in1=second[h][:], op=ALU.add)
+                                    in1=second[:, halves[h]], op=ALU.add)
         for h in range(2):
             nc.vector.tensor_tensor(out=scaled[h][:], in0=both[h][:], in1=out_slope[:, halves[h]], op=ALU.mult)
         for h in range(2):

@@ -98,36 +98,48 @@ def tile_attend_hvwriteread_kernel(tc, tab_words, tab_scales, w1, gain, pb, wo, 
         og_col = load_plain("og_col", og, F32)
         base_sb = load_plain("base_sb", base, F32)
 
+        identity = sb("identity", [P, P], F32)
+        make_identity(nc, identity[:])
+        zero_col = sb("zero_col", [P, 1], F32)
+        nc.scalar.activation(out=zero_col[:], in_=identity[:, 0:1], func=ACT.Silu, scale=0.0)
         w1_grouped = interleave("w1_grouped", w1_raw)
         tab_picked_words = gather_packed("tab_picked_words", tab_word_win, U16)
         tab_picked_scales = gather_packed("tab_picked_scales", tab_scale_win, U8)
         w1_codes, w1_scales = quantise("w1", w1_grouped)
 
         def first_layer(name, words, scales):
-            acc = psum.tile([P, J], F32, name=name)
+            acc = psum.tile([P, words.shape[1]], F32, name=name)
             nc.tensor.matmul_mx(out=acc[:], lhsT=w1_codes[:].bitcast(FP8X4), lhsT_scale=w1_scales[:],
-                                rhs=words[:].bitcast(FP4X4), rhs_scale=scales[:], start=True, stop=True)
+                                rhs=words.bitcast(FP4X4), rhs_scale=scales, start=True, stop=True)
             return acc
 
-        a = first_layer("a", tab_picked_words, tab_picked_scales)
+        halves = [slice(h * HALF, (h + 1) * HALF) for h in range(2)]
+        a = [first_layer("a%d" % h, tab_picked_words[:, halves[h]], tab_picked_scales[:, halves[h]]) for h in range(2)]
         dtab_picked_words = gather_packed("dtab_picked_words", dtab_word_win, U16)
         dtab_picked_scales = gather_packed("dtab_picked_scales", dtab_scale_win, U8)
-        ta = first_layer("ta", dtab_picked_words, dtab_picked_scales)
+        ta = first_layer("ta", dtab_picked_words[:], dtab_picked_scales[:])
 
-        gain_rows = affine("gain_rows", gain_col[:].to_broadcast([P, J]), 1.0)
         h1 = sb("h1", [P, J], F32)
-        nc.scalar.activation(out=h1[:], in_=a[:], func=ACT.Tanh)
-        nc.vector.tensor_tensor(out=pages["pg"][:].indirect(list2[:]), in0=h1[:], in1=gain_rows[:], op=ALU.mult)
+        h2 = sb("h2", [P, J], F32)
+        for h in range(2):
+            nc.scalar.activation(out=h1[:, halves[h]], in_=a[h][:], func=ACT.Tanh, bias=zero_col[:])
+        for h in range(2):
+            nc.scalar.activation(out=h2[:, halves[h]], in_=h1[:, halves[h]], func=ACT.Copy, scale=gain_col[:])
+        nc.vector.tensor_copy(out=pages["pg"][:].indirect(list2[:]), in_=h2[:])
 
+        half_gain = affine("half_gain", gain_col[:], 0.5)
+        neg_half_gain = affine("neg_half_gain", gain_col[:], -0.5)
         h1_sq = sb("h1_sq", [P, J], F32)
-        nc.scalar.activation(out=h1_sq[:], in_=h1[:], func=ACT.Square)
-        slope = affine("slope", h1_sq[:], -1.0, 1.0)
-        ta_gain = affine("ta_gain", ta[:], gain_col[:])
+        nc.gpsimd.tensor_tensor(out=h1_sq[:], in0=h1[:], in1=h1[:], op=ALU.mult)
+        gain_slope = sb("gain_slope", [P, J], F32)
+        nc.gpsimd.tensor_scalar(out=gain_slope[:], in0=h1_sq[:], scalar1=half_gain[:], scalar2=neg_half_gain[:],
+                                op0=ALU.mult, op1=ALU.add)
         dy_grouped = interleave("dy_grouped", dy_raw)
+        ta_m2 = affine("dy_raw", ta[:], -2.0)
+        xh2 = sb("xh2", [P, J], F32)
+        nc.gpsimd.tensor_tensor(out=xh2[:], in0=ta_m2[:], in1=gain_slope[:], op=ALU.mult)
         wo_grouped = interleave("wo_grouped", wo_raw)
 
-        identity = sb("identity", [P, P], F32)
-        make_identity(nc, identity[:])
         pb_turned = psum.tile([P, M // P, P], F32, name="pb_turned")
         for c in range(M // P):
             nc.tensor.transpose(pb_turned[:, c, :], pb_cols[:, c:c + 1].to_broadcast([P, P]), identity[:])
@@ -138,31 +150,32 @@ def tile_attend_hvwriteread_kernel(tc, tab_words, tab_scales, w1, gain, pb, wo, 
         wo_codes, wo_scales = quantise("wo", wo_grouped)
         s = sb("dy_grouped", [P, M], F32)
         nc.vector.tensor_tensor(out=s[:], in0=pages["pg"][:].indirect(list3[:]), in1=pb_rows[:], op=ALU.add)
-        curv = sb("wo_grouped", [P, J], F32)
-        nc.vector.scalar_tensor_tensor(out=curv[:], in0=ta[:], scalar=-2.0, in1=h1[:], op0=ALU.mult, op1=ALU.mult)
+        curv = sb("pb_rows", [P, J], F32)
+        nc.gpsimd.tensor_tensor(out=curv[:], in0=ta_m2[:], in1=h1[:], op=ALU.mult)
         c0 = psum.tile([P, M], F32, name="c0")
         nc.tensor.matmul_mx(out=c0[:], lhsT=wo_codes[:].bitcast(FP8X4), lhsT_scale=wo_scales[:],
                             rhs=dy_codes[:].bitcast(FP8X4), rhs_scale=dy_scales[:], start=True, stop=True)
-        nc.vector.tensor_tensor(out=pages["pg"][:].indirect(list2[:]), in0=ta_gain[:], in1=slope[:], op=ALU.mult)
+        nc.vector.tensor_copy(out=pages["pg"][:].indirect(list2[:]), in_=xh2[:])
 
-        neg_silu = sb("neg_silu", [P, M], F32)
-        nc.scalar.activation(out=neg_silu[:], in_=s[:], func=ACT.Silu, scale=-1.0)
+        c0_sb = affine("c0_sb", c0[:], 1.0)
         th = sb("th", [P, M], F32)
         nc.scalar.activation(out=th[:], in_=s[:], func=ACT.Tanh, scale=0.5)
+        neg_silu = sb("neg_silu", [P, M], F32)
+        nc.scalar.activation(out=neg_silu[:], in_=s[:], func=ACT.Silu, scale=-1.0)
+        sig2 = affine("sig2", th[:], 1.0, 1.0)
         half_q = affine("half_q", neg_silu[:], -0.5, 0.5)
-        out_gain = affine("out_gain", gain_col[:], og_col[:])
-        out_slope = affine("out_slope", slope[:], out_gain[:])
+        out_gain = affine("out_gain", og_col[:], -2.0)
+        out_slope = affine("out_slope", gain_slope[:], out_gain[:])
 
         c_sig2 = sb("c_sig2", [P, M], F32)
-        nc.vector.scalar_tensor_tensor(out=c_sig2[:], in0=th[:], scalar=1.0, in1=c0[:], op0=ALU.add, op1=ALU.mult)
-        e_less1 = sb("e_less1", [P, M], F32)
-        nc.vector.scalar_tensor_tensor(out=e_less1[:], in0=neg_silu[:], scalar=-1.0, in1=th[:], op0=ALU.add, op1=ALU.mult)
-        half_e = affine("half_e", e_less1[:], 0.5, 0.5)
+        nc.gpsimd.tensor_tensor(out=c_sig2[:], in0=sig2[:], in1=c0_sb[:], op=ALU.mult)
+        th_q = sb("th_q", [P, M], F32)
+        nc.gpsimd.tensor_tensor(out=th_q[:], in0=th[:], in1=half_q[:], op=ALU.mult)
+        half_e = affine("half_e", th_q[:], -1.0, 0.5)
         nc.vector.tensor_tensor(out=pages["s1"][:].indirect(list3[:]), in0=c_sig2[:], in1=half_q[:], op=ALU.mult)
         xs_c = sb("xs_c", [P, M], F32)
         nc.vector.tensor_tensor(out=xs_c[:], in0=pages["pg"][:].indirect(list3[:]), in1=c_sig2[:], op=ALU.mult)
 
-        halves = [slice(h * HALF, (h + 1) * HALF) for h in range(2)]
         half_lists = [list2[:, h * HALF // 16:(h + 1) * HALF // 16] for h in range(2)]
         both = [sb("both%d" % h, [P, HALF], F32) for h in range(2)]
         scaled = [sb("scaled%d" % h, [P, HALF], F32) for h in range(2)]

@@ -150,8 +150,10 @@ def tile_attend_hvwriteread_kernel(tc, tab_words, tab_scales, w1, gain, pb, wo, 
         wo_codes, wo_scales = quantise("wo", wo_grouped)
         s = sb("dy_grouped", [P, M], F32)
         nc.vector.tensor_tensor(out=s[:], in0=pages["pg"][:].indirect(list3[:]), in1=pb_rows[:], op=ALU.add)
+        out_gain = affine("out_gain", og_col[:], -2.0)
+        h1_gain = affine("h1_gain", h1[:], out_gain[:])
         curv = sb("pb_rows", [P, J], F32)
-        nc.gpsimd.tensor_tensor(out=curv[:], in0=ta_m2[:], in1=h1[:], op=ALU.mult)
+        nc.gpsimd.tensor_tensor(out=curv[:], in0=xh2[:], in1=h1_gain[:], op=ALU.mult)
         c0 = psum.tile([P, M], F32, name="c0")
         nc.tensor.matmul_mx(out=c0[:], lhsT=wo_codes[:].bitcast(FP8X4), lhsT_scale=wo_scales[:],
                             rhs=dy_codes[:].bitcast(FP8X4), rhs_scale=dy_scales[:], start=True, stop=True)
@@ -164,30 +166,40 @@ def tile_attend_hvwriteread_kernel(tc, tab_words, tab_scales, w1, gain, pb, wo, 
         nc.scalar.activation(out=neg_silu[:], in_=s[:], func=ACT.Silu, scale=-1.0)
         sig2 = affine("sig2", th[:], 1.0, 1.0)
         half_q = affine("half_q", neg_silu[:], -0.5, 0.5)
-        out_gain = affine("out_gain", og_col[:], -2.0)
         out_slope = affine("out_slope", gain_slope[:], out_gain[:])
 
-        c_sig2 = sb("c_sig2", [P, M], F32)
-        nc.gpsimd.tensor_tensor(out=c_sig2[:], in0=sig2[:], in1=c0_sb[:], op=ALU.mult)
-        th_q = sb("th_q", [P, M], F32)
-        nc.gpsimd.tensor_tensor(out=th_q[:], in0=th[:], in1=half_q[:], op=ALU.mult)
+        def product(name, x, y):
+            dst = sb(name, list(x.shape), F32)
+            nc.gpsimd.tensor_tensor(out=dst[:], in0=x[:], in1=y[:], op=ALU.mult)
+            return dst
+
+        c_sig2 = product("c_sig2", sig2, c0_sb)
+        th_q = product("th_q", th, half_q)
         half_e = affine("half_e", th_q[:], -1.0, 0.5)
         nc.vector.tensor_tensor(out=pages["s1"][:].indirect(list3[:]), in0=c_sig2[:], in1=half_q[:], op=ALU.mult)
         xs_c = sb("xs_c", [P, M], F32)
         nc.vector.tensor_tensor(out=xs_c[:], in0=pages["pg"][:].indirect(list3[:]), in1=c_sig2[:], op=ALU.mult)
-
         half_lists = [list2[:, h * HALF // 16:(h + 1) * HALF // 16] for h in range(2)]
-        both = [sb("both%d" % h, [P, HALF], F32) for h in range(2)]
-        scaled = [sb("scaled%d" % h, [P, HALF], F32) for h in range(2)]
+
+        second = sb("th_q", [P, J], F32)
+
+        def second_term(h):
+            nc.vector.tensor_tensor(out=second[:, halves[h]], in0=pages["s1"][:].indirect(half_lists[h]),
+                                    in1=curv[:, halves[h]], op=ALU.mult)
+
+        second_term(0)
+        xds = sb("xds", [P, M], F32)
+        nc.vector.tensor_tensor(out=xds[:], in0=xs_c[:], in1=half_e[:], op=ALU.mult)
+        second_term(1)
+        nc.vector.tensor_copy(out=pages["xs1"][:].indirect(list3[:]), in_=xds[:])
+        second_base = sb("second_base", [P, J], F32)
+        nc.gpsimd.tensor_tensor(out=second_base[:], in0=second[:], in1=base_sb[:], op=ALU.add)
+
+        first = [sb("first%d" % h, [P, HALF], F32) for h in range(2)]
         result = [sb("result%d" % h, [P, HALF], F32) for h in range(2)]
-        second = sb("second", [P, J], F32)
-        nc.vector.tensor_tensor(out=second[:], in0=pages["s1"][:].indirect(list2[:]), in1=curv[:], op=ALU.mult)
-        nc.vector.tensor_tensor(out=pages["xs1"][:].indirect(list3[:]), in0=xs_c[:], in1=half_e[:], op=ALU.mult)
         for h in range(2):
-            nc.vector.tensor_tensor(out=both[h][:], in0=pages["xs1"][:].indirect(half_lists[h]),
-                                    in1=second[:, halves[h]], op=ALU.add)
+            nc.vector.tensor_tensor(out=first[h][:], in0=pages["xs1"][:].indirect(half_lists[h]),
+                                    in1=out_slope[:, halves[h]], op=ALU.mult)
         for h in range(2):
-            nc.vector.tensor_tensor(out=scaled[h][:], in0=both[h][:], in1=out_slope[:, halves[h]], op=ALU.mult)
-        for h in range(2):
-            nc.vector.tensor_tensor(out=result[h][:], in0=scaled[h][:], in1=base_sb[:, halves[h]], op=ALU.add)
+            nc.vector.tensor_tensor(out=result[h][:], in0=first[h][:], in1=second_base[:, halves[h]], op=ALU.add)
             nc.sync.dma_start(out=out[:, halves[h]], in_=result[h][:])

from contextlib import ExitStack

import concourse.mybir as mybir
from concourse.masks import make_identity

K, R, F, T, J, U, M = 512, 128, 512, 2048, 512, 1024, 256
P = 128
PACK = 4
HALF = J // 2

FLOPS = 2 * K * R * J * 2 + 2 * F * R * M

F32 = mybir.dt.float32
BF16 = mybir.dt.bfloat16
I32 = mybir.dt.int32
U32 = mybir.dt.uint32
U16 = mybir.dt.uint16
U8 = mybir.dt.uint8
FP8X4 = mybir.dt.float8_e4m3fn_x4
FP4X4 = mybir.dt.float4_e2m1fn_x4
ALU = mybir.AluOpType
ACT = mybir.ActivationFunctionType


def tile_attend_hvwriteread_kernel(tc, tab_words, tab_scales, w1, gain, pb, wo, dy, dtab_words, dtab_scales,
                                    og, base, offs, offs2, offs3, out):
    nc = tc.nc
    with ExitStack() as ctx:
        pool = ctx.enter_context(tc.tile_pool(name="sbuf", bufs=1))
        psum = ctx.enter_context(tc.psum_pool(name="psum", bufs=1))

        def sb(name, shape, dtype):
            return pool.tile(shape, dtype, name=name, align_bytes=64)

        def load_words(name, words):
            window = sb(name, [P, T], U16)
            nc.sync.dma_start(out=window[:].bitcast(I32), in_=words[0].bitcast(I32))
            return window

        def load_scales(queue, window, scales):
            for row in range(4):
                queue.dma_start(out=window[row:P:32, :].bitcast(I32), in_=scales[0, row:16:4, :].bitcast(I32))

        def load_rows(name, rows):
            raw = sb(name, [P, PACK, rows.shape[1]], F32)
            nc.sync.dma_start(out=raw[:], in_=rows.rearrange("(p t) c -> p t c", t=PACK))
            return raw

        def load_plain(name, src, dtype, queue=nc.sync):
            tile = sb(name, list(src.shape), dtype)
            queue.dma_start(out=tile[:], in_=src)
            return tile

        def interleave(name, raw):
            grouped = sb(name, [P, raw.shape[2], PACK], BF16)
            nc.scalar.copy(out=grouped[:], in_=raw[:].rearrange("p t c -> p c t"))
            return grouped

        def quantise(name, grouped):
            width = grouped.shape[1]
            codes = sb(name + "_codes", [P, width], U32)
            scales = sb(name + "_scales", [P, width], U8)
            nc.vector.quantize_mx(out=codes[:].bitcast(FP8X4), scales=scales[:],
                                  in_=grouped[:].rearrange("p c t -> p (c t)"))
            return codes, scales

        def gather_packed(name, window, dtype):
            picked = sb(name, [P, J], dtype)
            nc.vector.tensor_copy(out=picked[:], in_=window[:].indirect(list1[:]))
            return picked

        def affine(name, src, scale, bias=0.0):
            dst = sb(name, list(src.shape), F32)
            nc.scalar.activation(out=dst[:], in_=src, func=ACT.Copy, scale=scale, bias=bias)
            return dst

        tab_scale_win = sb("tab_scale_win", [P, T], U8)
        dtab_scale_win = sb("dtab_scale_win", [P, T], U8)
        nc.vector.memset(tab_scale_win[:].bitcast(I32), 0)
        nc.vector.memset(dtab_scale_win[:].bitcast(I32), 0)
        pages = {}
        for name in ("pg", "s1", "xs1"):
            pages[name] = sb(name, [P, U], F32)
            nc.vector.memset(pages[name][:], 0.0)

        list1 = load_plain("list1", offs, U16)
        tab_word_win = load_words("tab_word_win", tab_words)
        w1_raw = load_rows("w1_raw", w1)
        load_scales(nc.sync, tab_scale_win, tab_scales)
        gain_col = load_plain("gain_col", gain, F32)
        dtab_word_win = load_words("dtab_word_win", dtab_words)
        load_scales(nc.sync, dtab_scale_win, dtab_scales)
        list2 = load_plain("list2", offs2, U16)
        dy_raw = load_rows("dy_raw", dy)
        wo_raw = load_rows("wo_raw", wo)
        list3 = load_plain("list3", offs3, U16)
        pb_cols = load_plain("pb_cols", pb[0].rearrange("(p c) -> p c", p=P), F32)
        og_col = load_plain("og_col", og, F32)
        base_sb = load_plain("base_sb", base, F32)

        identity = sb("identity", [P, P], F32)
        make_identity(nc, identity[:])
        zero_col = sb("zero_col", [P, 1], F32)
        nc.scalar.activation(out=zero_col[:], in_=identity[:, 0:1], func=ACT.Silu, scale=0.0)
        w1_grouped = interleave("w1_grouped", w1_raw)
        tab_picked_words = gather_packed("tab_picked_words", tab_word_win, U16)
        tab_picked_scales = gather_packed("tab_picked_scales", tab_scale_win, U8)
        w1_codes, w1_scales = quantise("w1", w1_grouped)

        def first_layer(name, words, scales):
            acc = psum.tile([P, words.shape[1]], F32, name=name)
            nc.tensor.matmul_mx(out=acc[:], lhsT=w1_codes[:].bitcast(FP8X4), lhsT_scale=w1_scales[:],
                                rhs=words.bitcast(FP4X4), rhs_scale=scales, start=True, stop=True)
            return acc

        halves = [slice(h * HALF, (h + 1) * HALF) for h in range(2)]
        a = [first_layer("a%d" % h, tab_picked_words[:, halves[h]], tab_picked_scales[:, halves[h]]) for h in range(2)]
        dtab_picked_words = gather_packed("dtab_picked_words", dtab_word_win, U16)
        dtab_picked_scales = gather_packed("dtab_picked_scales", dtab_scale_win, U8)
        ta = first_layer("ta", dtab_picked_words[:], dtab_picked_scales[:])

        h1 = sb("h1", [P, J], F32)
        h2 = sb("h2", [P, J], F32)
        for h in range(2):
            nc.scalar.activation(out=h1[:, halves[h]], in_=a[h][:], func=ACT.Tanh, bias=zero_col[:])
        for h in range(2):
            nc.scalar.activation(out=h2[:, halves[h]], in_=h1[:, halves[h]], func=ACT.Copy, scale=gain_col[:])
        nc.vector.tensor_copy(out=pages["pg"][:].indirect(list2[:]), in_=h2[:])

        half_gain = affine("half_gain", gain_col[:], 0.5)
        neg_half_gain = affine("neg_half_gain", gain_col[:], -0.5)
        h1_sq = sb("h1_sq", [P, J], F32)
        nc.gpsimd.tensor_tensor(out=h1_sq[:], in0=h1[:], in1=h1[:], op=ALU.mult)
        gain_slope = sb("gain_slope", [P, J], F32)
        nc.gpsimd.tensor_scalar(out=gain_slope[:], in0=h1_sq[:], scalar1=half_gain[:], scalar2=neg_half_gain[:],
                                op0=ALU.mult, op1=ALU.add)
        dy_grouped = interleave("dy_grouped", dy_raw)
        ta_m2 = affine("dy_raw", ta[:], -2.0)
        xh2 = sb("xh2", [P, J], F32)
        nc.gpsimd.tensor_tensor(out=xh2[:], in0=ta_m2[:], in1=gain_slope[:], op=ALU.mult)
        wo_grouped = interleave("wo_grouped", wo_raw)

        pb_turned = psum.tile([P, M // P, P], F32, name="pb_turned")
        for c in range(M // P):
            nc.tensor.transpose(pb_turned[:, c, :], pb_cols[:, c:c + 1].to_broadcast([P, P]), identity[:])
        pb_rows = sb("pb_rows", [P, M], F32)
        nc.scalar.copy(out=pb_rows[:].rearrange("p (n c) -> p n c", c=M // P), in_=pb_turned[:].rearrange("p c n -> p n c"))

        dy_codes, dy_scales = quantise("dy", dy_grouped)
        wo_codes, wo_scales = quantise("wo", wo_grouped)
        s = sb("dy_grouped", [P, M], F32)
        nc.vector.tensor_tensor(out=s[:], in0=pages["pg"][:].indirect(list3[:]), in1=pb_rows[:], op=ALU.add)
        out_gain = affine("out_gain", og_col[:], -2.0)
        h1_gain = affine("h1_gain", h1[:], out_gain[:])
        curv = sb("pb_rows", [P, J], F32)
        nc.gpsimd.tensor_tensor(out=curv[:], in0=xh2[:], in1=h1_gain[:], op=ALU.mult)
        c0 = psum.tile([P, M], F32, name="c0")
        nc.tensor.matmul_mx(out=c0[:], lhsT=wo_codes[:].bitcast(FP8X4), lhsT_scale=wo_scales[:],
                            rhs=dy_codes[:].bitcast(FP8X4), rhs_scale=dy_scales[:], start=True, stop=True)
        nc.vector.tensor_copy(out=pages["pg"][:].indirect(list2[:]), in_=xh2[:])

        c0_sb = affine("c0_sb", c0[:], 1.0)
        th = sb("th", [P, M], F32)
        nc.scalar.activation(out=th[:], in_=s[:], func=ACT.Tanh, scale=0.5)
        neg_silu = sb("neg_silu", [P, M], F32)
        nc.scalar.activation(out=neg_silu[:], in_=s[:], func=ACT.Silu, scale=-1.0)
        sig2 = affine("sig2", th[:], 1.0, 1.0)
        half_q = affine("half_q", neg_silu[:], -0.5, 0.5)
        out_slope = affine("out_slope", gain_slope[:], out_gain[:])

        def product(name, x, y):
            dst = sb(name, list(x.shape), F32)
            nc.gpsimd.tensor_tensor(out=dst[:], in0=x[:], in1=y[:], op=ALU.mult)
            return dst

        c_sig2 = product("c_sig2", sig2, c0_sb)
        th_q = product("th_q", th, half_q)
        half_e = affine("half_e", th_q[:], -1.0, 0.5)
        nc.vector.tensor_tensor(out=pages["s1"][:].indirect(list3[:]), in0=c_sig2[:], in1=half_q[:], op=ALU.mult)
        xs_c = sb("xs_c", [P, M], F32)
        nc.vector.tensor_tensor(out=xs_c[:], in0=pages["pg"][:].indirect(list3[:]), in1=c_sig2[:], op=ALU.mult)
        half_lists = [list2[:, h * HALF // 16:(h + 1) * HALF // 16] for h in range(2)]

        second = sb("th_q", [P, J], F32)

        def second_term(h):
            nc.vector.tensor_tensor(out=second[:, halves[h]], in0=pages["s1"][:].indirect(half_lists[h]),
                                    in1=curv[:, halves[h]], op=ALU.mult)

        second_term(0)
        xds = sb("xds", [P, M], F32)
        nc.vector.tensor_tensor(out=xds[:], in0=xs_c[:], in1=half_e[:], op=ALU.mult)
        second_term(1)
        nc.vector.tensor_copy(out=pages["xs1"][:].indirect(list3[:]), in_=xds[:])
        second_base = sb("second_base", [P, J], F32)
        nc.gpsimd.tensor_tensor(out=second_base[:], in0=second[:], in1=base_sb[:], op=ALU.add)

        first = [sb("first%d" % h, [P, HALF], F32) for h in range(2)]
        result = [sb("result%d" % h, [P, HALF], F32) for h in range(2)]
        for h in range(2):
            nc.vector.tensor_tensor(out=first[h][:], in0=pages["xs1"][:].indirect(half_lists[h]),
                                    in1=out_slope[:, halves[h]], op=ALU.mult)
        for h in range(2):
            nc.vector.tensor_tensor(out=result[h][:], in0=first[h][:], in1=second_base[:, halves[h]], op=ALU.add)
            nc.sync.dma_start(out=out[:, halves[h]], in_=result[h][:])
